import numpy as np, ml_dtypes
CORES = [2,3,42,43,82,83,122,123]
N = 8
GR, GC = 2, 4
L, KA, KB, F = 4, 1, 2, 32
def setup_inputs(rng):
    return {"a": rng.standard_normal((N, 128, KA * 128), dtype=np.float32).astype(ml_dtypes.bfloat16), "b": rng.standard_normal((N, 128, KB * F), dtype=np.float32).astype(ml_dtypes.bfloat16)}
def setup_inputs_big(rng):
    d = setup_inputs(rng)
    for k in ("a", "b"): d[k] = (d[k].astype(np.float32) * 1024.0).astype(d[k].dtype)
    return d
def setup_inputs_small(rng):
    d = setup_inputs(rng)
    for k in ("a", "b"): d[k] = (d[k].astype(np.float32) * (1 / 1024.0)).astype(d[k].dtype)
    return d
def setup_inputs_apart(rng):
    d = setup_inputs(rng)
    f = (10.0 ** rng.permutation(np.linspace(-1.5, 1.5, N))).astype(np.float32).reshape(N, 1, 1)
    for k in ("a", "b"): d[k] = (d[k].astype(np.float32) * f).astype(d[k].dtype)
    return d
def reference(a, b):
    A, B = a.astype(np.float64), b.astype(np.float64)
    y = np.zeros((N, 128, F))
    for i in range(GR):
        for j in range(GC):
            for k in range(L):
                At = A[i * GC + k // KA][:, 128 * (k % KA):128 * (k % KA) + 128]
                Bt = B[(k // KB) * GC + j][:, F * (k % KB):F * (k % KB) + F]
                y[i * GC + j] += At.T @ Bt
    return {"y": y.astype(ml_dtypes.bfloat16 if a.dtype != np.float64 else np.float64)}

from concourse.bass import DstId, RemoteDMATransfer

GR, GC = 2, 4
L, F = 4, 32
KB = 2

SCRATCH = {
    "A": ("sbuf", [128, L * 128], "bfloat16"),
    "B": ("sbuf", [128, L * F], "bfloat16"),
    "acc": ("psum", [128, F], "float32"),
    "ysb": ("sbuf", [128, F], "bfloat16"),
}
SEMAPHORES = ["lda", "ldb", "ak0", "ak1", "ak2", "ak3", "bin", "sent", "mm", "cp", "st"]


def _bits(mask):
    return bin(mask).count("1")


def rank_program(g, core, T, topo):
    rank = T.rank_of(core)
    if rank is None:
        return
    i, j = divmod(rank, GC)
    S = T.sem

    def a_slot(k):
        return T.A[:, 128 * k:128 * (k + 1)]

    def b_half(r):
        return T.B[:, KB * F * r:KB * F * (r + 1)]

    g.sync.dma_start(a_slot(j), T.a[:, :]).then_inc(S.lda, 16)
    g.scalar.dma_start(b_half(i), T.b[:, :]).then_inc(S.ldb, 16)

    row = [T.cores[i * GC + k] for k in range(GC)]
    near = [c for c in row if c != core and topo.chip(c) == topo.chip(core)]
    far = [c for c in row if topo.chip(c) != topo.chip(core)]
    col = T.cores[(1 - i) * GC + j]
    for c in near + far + [col]:
        assert topo.may_write(core, c)
    m_out = topo.mask(core, col)
    for c in far:
        m_out &= topo.mask(core, c)
    m_in = {}
    for c in near:
        rest = topo.mask(core, c) & ~m_out
        m_in[c] = rest if rest else topo.mask(core, c)

    def dst(c):
        rid, pid, _ = topo.addr(c)
        return DstId(rid=rid, pnc=pid)

    sent = 0
    my_sem = S["ak%d" % j]
    g.wait_ge(S.lda, 16)
    if far:
        g.remote_dma_fused(
            [RemoteDMATransfer(dst_ids=[dst(c) for c in far], dma_engine_mask=m_out, remote_sem=my_sem,
                               srcs=[a_slot(j)], dsts=[a_slot(j) for _ in far], alu_op=0)],
            local_sem=S.sent)
        sent += _bits(m_out)
    g.wait_ge(S.ldb, 16)
    rid, pid, _ = topo.addr(col)
    g.remote_dma(b_half(i), b_half(i), S.bin, S.sent, pid, rid, m_out)
    sent += _bits(m_out)
    for c in near:
        rid, pid, _ = topo.addr(c)
        g.remote_dma(a_slot(j), a_slot(j), my_sem, S.sent, pid, rid, m_in[c])
        sent += _bits(m_in[c])

    def a_need(k):
        c = row[k]
        if c == core:
            return (0, "lda", 16)
        if c in near:
            rest = topo.mask(c, core) & ~topo.mask(c, T.cores[(1 - i) * GC + k])
            return (1, "ak%d" % k, _bits(rest if rest else topo.mask(c, core)))
        return (3, "ak%d" % k, _bits(topo.mask(c, core)))

    def b_need(k):
        if k // KB == i:
            return (0, "ldb", 16)
        return (2, "bin", _bits(topo.mask(col, core)))

    order = sorted(range(L), key=lambda k: (max(a_need(k)[0], b_need(k)[0]), k))
    waited = set()
    for n, k in enumerate(order):
        for _, name, cnt in (a_need(k), b_need(k)):
            if name not in waited:
                g.tensor.wait_ge(S[name], cnt)
                waited.add(name)
        g.tensor.matmul(T.acc[:, :], a_slot(k), T.B[:, F * k:F * (k + 1)],
                        n == 0, n == L - 1).then_inc(S.mm, 1)

    g.vector.wait_ge(S.mm, L)
    g.vector.tensor_copy(T.ysb[:, :], T.acc[:, :]).then_inc(S.cp, 1)
    g.sync.wait_ge(S.cp, 1)
    g.sync.dma_start(T.y[:, :], T.ysb[:, :]).then_inc(S.st, 16)
    g.sync.wait_ge(S.st, 16)
    g.wait_ge(S.sent, sent)
